import numpy as np
import ml_dtypes


def mxq(x, axis, fmt="e4m3"):
    dtype, down = {"e4m3": (ml_dtypes.float8_e4m3fn, 7), "e5m2": (ml_dtypes.float8_e5m2, 14)}[fmt]
    v = np.moveaxis(np.asarray(x, np.float32).astype(ml_dtypes.bfloat16).astype(np.float64), axis, -1)
    blocks = v.reshape(v.shape[:-1] + (-1, 32))
    amax = np.abs(blocks).max(-1, keepdims=True)
    byte = np.maximum(np.where(amax > 0, np.frexp(amax)[1] - 1 + 127, 0) - down, 1)
    scale = np.exp2(byte - 127.0)
    codes = (blocks / scale).astype(np.float32).astype(dtype).astype(np.float64)
    return np.moveaxis((codes * scale).reshape(v.shape), -1, axis)


WIDE = False


def mx_kscale(k):
    if not WIDE:
        return np.ones(k)
    levels = np.array([10, -10, 5, -5, 0])
    if k % 512:
        return np.exp2(np.random.permutation(np.resize(levels, k // 32))).repeat(32)
    a = np.empty((k // 512, 16))
    for p in range(k // 512):
        a[p, :8] = np.random.permutation(np.resize(levels, 8))
        for g in range(8):
            far = levels[np.abs(levels - a[p, g]) >= 10]
            a[p, g + 8] = far[np.random.randint(len(far))]
    return np.exp2(a.ravel()).repeat(32)


def f64(x):
    return np.asarray(x).astype(np.float64)


def striped(idx):
    return np.tile(idx.reshape(-1, 16).T, (8, 1)).astype(np.uint16)


def unstriped(offs):
    return offs[:16].T.reshape(-1).astype(np.int64)


def striped8(idx):
    return np.concatenate([x.reshape(-1, 16).T for x in idx]).astype(np.uint16)


def runs(offs, k):
    lists = np.stack([offs[16 * r : 16 * r + 16].T.reshape(-1) for r in range(8)]).astype(np.int64)
    return lists[np.arange(k) % 512 // 64]


def pack_weight(w):
    k, n = w.shape
    w = f64(np.asarray(w, np.float32).astype(ml_dtypes.bfloat16)).reshape(k // 32, 32, n)
    amax = np.abs(w).max(1)
    byte = np.clip(np.where(amax > 0, np.frexp(amax)[1] - 1 + 127 - 7, 1), 1, 254)
    scaled = (w * np.exp2(127.0 - byte)[:, None, :]).reshape(k, n).astype(np.float32)
    words = np.ascontiguousarray(scaled.reshape(k // 512, 128, 4, n).transpose(0, 1, 3, 2)).astype(ml_dtypes.float8_e4m3fn).view(np.uint8)
    return words, np.ascontiguousarray(byte.astype(np.uint8).reshape(k // 512, 16, n))


def unpack_weight(words, scales):
    g, p, n, _ = words.shape
    vals = np.ascontiguousarray(words).view(ml_dtypes.float8_e4m3fn).astype(np.float64) * np.repeat(np.exp2(scales.astype(np.float64) - 127.0), 8, axis=1)[..., None]
    return vals.transpose(0, 1, 3, 2).reshape(g * 512, n)


def sigmoid(v):
    return 1.0 / (1.0 + np.exp(-np.maximum(v, -700.0)))


K, T, S, H, U = 512, 2048, 512, 512, 1024


def setup_inputs():
    n = np.random.standard_normal
    s = mx_kscale(K)[:, None]
    u = mx_kscale(S)
    packed_xT = pack_weight(n((K, T)) * s)
    return {
        "x_words": packed_xT[0],
        "x_scales": packed_xT[1],
        "w1": (n((K, H)) / np.sqrt(K) / s).astype(np.float32),
        "mem": n((H, U)).astype(np.float32),
        "ga": (np.random.uniform(0.5, 1.5, (H, 1)) * u[:, None]).astype(np.float32),
        "gb": (np.random.uniform(0.5, 1.5, (H, 1)) / u[:, None]).astype(np.float32),
        "offs": striped(np.random.permutation(T)[:S]),
        "n1": striped8(np.stack([np.random.permutation(S) for _ in range(8)])),
        "n2": striped8(np.stack([np.random.permutation(S) for _ in range(8)])),
        "n3": striped8(np.stack([np.random.permutation(U)[:S] for _ in range(8)])),
        "n4": striped8(np.stack([np.random.permutation(U) for _ in range(8)])),
        "n5": striped8(np.stack([np.random.permutation(U) for _ in range(8)])),
    }


def reference(x_words, x_scales, w1, mem, ga, gb, offs, n1, n2, n3, n4, n5):
    xq = unpack_weight(x_words, x_scales)[:, unstriped(offs)]
    y = mxq(f64(w1), 0, "e4m3").T @ xq
    sq = (y) ** 2
    z = f64(ga) * ((y[np.arange(H)[:, None], runs(n2, H)]) / (np.sqrt(sq + sq[np.arange(H)[:, None], runs(n1, H)] + 0.25)))
    old = f64(mem)[np.arange(H)[:, None], runs(n3, H)]
    nw = old + sigmoid(y) * (y - old)
    pg = f64(mem).copy()
    pg[np.arange(H)[:, None], runs(n3, H)] = nw
    z2 = f64(gb) * pg
    s = 0.0625 * ((mxq(z, 0, "e4m3").T @ mxq(z2, 0, "e4m3")))
    return (s[np.arange(S)[:, None], runs(n4, S)]) * (s[np.arange(S)[:, None], runs(n5, S)])

@@ -1,0 +1,307 @@
+from contextlib import ExitStack
+
+import concourse.mybir as mybir
+from concourse.masks import make_identity
+
+K, T, S, H, U = 512, 2048, 512, 512, 1024
+FLOPS = 2 * K * H * S + 2 * H * S * U
+
+F32 = mybir.dt.float32
+BF16 = mybir.dt.bfloat16
+I32 = mybir.dt.int32
+U32 = mybir.dt.uint32
+U16 = mybir.dt.uint16
+U8 = mybir.dt.uint8
+FP8X4 = mybir.dt.float8_e4m3fn_x4
+ACT = mybir.ActivationFunctionType
+ALU = mybir.AluOpType
+
+P = 128
+PACK = 4
+W_VECTOR = 44
+HALF_H = H // 2
+HALF_S = S // 2
+HALF_U = U // 2
+
+
+def tile_picked_selfrmspagetprod_none_p_kernel(
+    tc, x_words, x_scales, w1, mem, ga, gb, offs, n1, n2, n3, n4, n5, out
+):
+    nc = tc.nc
+    with ExitStack() as ctx:
+        lists = ctx.enter_context(tc.tile_pool(name="lists", bufs=1))
+        keep = ctx.enter_context(tc.tile_pool(name="keep", bufs=1))
+        psum = ctx.enter_context(tc.psum_pool(name="psum", bufs=1))
+
+        def entries(lst, start, count):
+            return lst[:, start // 16 : (start + count) // 16]
+
+        def row_tiles(name, width, dtype):
+            return [keep.tile([P, width], dtype, name="%s%d" % (name, t), align_bytes=64) for t in range(PACK)]
+
+        def bank(b):
+            return psum.tile([P, 512], F32, name="bank%d" % b)
+
+        offs_sb = lists.tile([P, S // 16], U16, name="offs_sb")
+        n1_sb = lists.tile([P, S // 16], U16, name="n1_sb")
+        n2_sb = lists.tile([P, S // 16], U16, name="n2_sb")
+        n3_sb = lists.tile([P, S // 16], U16, name="n3_sb")
+        n4_sb = lists.tile([P, U // 16], U16, name="n4_sb")
+        n5_sb = lists.tile([P, U // 16], U16, name="n5_sb")
+
+        xw_all = keep.tile([P, T], U32, align_bytes=64, name="xw_all")
+        xs_all = keep.tile([P, T], U8, align_bytes=64, name="xs_all")
+        w_raw = [keep.tile([P, PACK, HALF_H], F32, align_bytes=64, name="w_raw%d" % h) for h in range(2)]
+        ga_sb = keep.tile([P, PACK], F32, name="ga_sb")
+        gb_sb = keep.tile([P, PACK], F32, name="gb_sb")
+        page = row_tiles("page", U, F32)
+        mem_rows = mem.rearrange("(p t) w -> t p w", t=PACK)
+        out_rows = out.rearrange("(p t) w -> t p w", t=PACK)
+
+        nc.vector.memset(xs_all[:].bitcast(I32), 0)
+        nc.sync.dma_start(out=offs_sb[:], in_=offs)
+        nc.sync.dma_start(out=xw_all[:].bitcast(I32), in_=x_words[0].rearrange("p n r -> p (n r)").bitcast(I32))
+        for q in range(4):
+            nc.sync.dma_start(
+                out=xs_all[32 * q : 32 * q + 4, :].bitcast(I32), in_=x_scales[0, 4 * q : 4 * q + 4, :].bitcast(I32)
+            )
+        w_rows = w1.rearrange("(p j) c -> p j c", j=PACK)
+        for h in range(2):
+            nc.sync.dma_start(out=w_raw[h][:], in_=w_rows[:, :, h * HALF_H : (h + 1) * HALF_H])
+        nc.sync.dma_start(out=n3_sb[:], in_=n3)
+        nc.sync.dma_start(out=page[0][:], in_=mem_rows[0])
+        nc.sync.dma_start(out=page[1][:], in_=mem_rows[1])
+        nc.sync.dma_start(out=n1_sb[:], in_=n1)
+        nc.sync.dma_start(out=page[2][:], in_=mem_rows[2])
+        nc.sync.dma_start(out=page[3][:], in_=mem_rows[3])
+        nc.sync.dma_start(out=n2_sb[:], in_=n2)
+        nc.sync.dma_start(out=n4_sb[:], in_=n4)
+        nc.sync.dma_start(out=n5_sb[:], in_=n5)
+        nc.gpsimd.dma_start(out=gb_sb[:], in_=gb.rearrange("(p t) o -> p (t o)", t=PACK))
+        nc.gpsimd.dma_start(out=ga_sb[:], in_=ga.rearrange("(p t) o -> p (t o)", t=PACK))
+        ident = keep.tile([P, P], F32, align_bytes=64, name="ident")
+        make_identity(nc, ident[:])
+        sixteenth = keep.tile([P, 1], F32, name="sixteenth")
+        nc.gpsimd.memset(sixteenth[:], 0.0625)
+
+        w_bf = keep.tile([P, PACK, P, PACK], BF16, align_bytes=64, name="w_bf")
+        w_dst = w_bf[:].rearrange("p t m j -> p m j t")
+        w_src = [w_raw[h][:].rearrange("p j (m t) -> p m j t", t=PACK) for h in range(2)]
+        xw = keep.tile([P, S], U32, align_bytes=64, name="xw")
+        xs = keep.tile([P, S], U8, align_bytes=64, name="xs")
+        nc.vector.tensor_copy(out=xw[:], in_=xw_all[:].indirect(offs_sb[:]))
+        nc.vector.tensor_copy(out=xs[:], in_=xs_all[:].indirect(offs_sb[:]))
+        nc.scalar.copy(out=w_dst[:, 0:64], in_=w_src[0])
+        nc.vector.tensor_copy(out=w_dst[:, 64 : 64 + W_VECTOR], in_=w_src[1][:, 0:W_VECTOR])
+        nc.scalar.copy(out=w_dst[:, 64 + W_VECTOR : P], in_=w_src[1][:, W_VECTOR:64])
+        w_codes = keep.tile([P, H], U32, align_bytes=64, name="w_codes")
+        w_scale = keep.tile([P, H], U8, align_bytes=64, name="w_scale")
+        y_ps = [bank(4 + t) for t in range(PACK)]
+        for t in range(PACK):
+            feats = slice(t * P, (t + 1) * P)
+            nc.vector.quantize_mx(
+                out=w_codes[:, feats].bitcast(FP8X4), scales=w_scale[:, feats], in_=w_bf[:, t].rearrange("p m j -> p (m j)")
+            )
+            nc.tensor.matmul_mx(
+                out=y_ps[t][:],
+                lhsT=w_codes[:, feats].bitcast(FP8X4),
+                lhsT_scale=w_scale[:, feats],
+                rhs=xw[:].bitcast(FP8X4),
+                rhs_scale=xs[:],
+                start=True,
+                stop=True,
+            )
+
+        hy = row_tiles("hy", S, F32)
+        th = row_tiles("th", S, F32)
+        old = row_tiles("old", S, F32)
+        diff = row_tiles("diff", S, F32)
+        step = row_tiles("step", S, F32)
+        sq = row_tiles("sq", S, F32)
+        sq_n1 = row_tiles("sqn1", S, F32)
+        inv_t = row_tiles("invT", S, F32)
+        hy_n2 = row_tiles("hyn2", S, F32)
+        z_rows = keep.tile([P, PACK, S], BF16, align_bytes=64, name="z_rows")
+        z2_rows = keep.tile([P, PACK, U], BF16, align_bytes=64, name="z2_rows")
+        den_ps = {}
+        inv_ps = {}
+
+        def fetch_y(t):
+            nc.scalar.activation(out=hy[t][:], in_=y_ps[t][:], func=ACT.Copy, scale=0.5)
+            nc.scalar.activation(out=th[t][:], in_=y_ps[t][:], func=ACT.Tanh, scale=0.5)
+
+        def write_page(t):
+            nc.vector.scalar_tensor_tensor(
+                out=diff[t][:], in0=old[t][:], scalar=-0.5, in1=hy[t][:], op0=ALU.mult, op1=ALU.add
+            )
+            nc.vector.scalar_tensor_tensor(
+                out=step[t][:], in0=th[t][:], scalar=1.0, in1=diff[t][:], op0=ALU.add, op1=ALU.mult
+            )
+            nc.vector.tensor_tensor(out=page[t][:].indirect(n3_sb[:]), in0=step[t][:], in1=old[t][:], op=ALU.add)
+
+        def fetch_old(t):
+            nc.scalar.activation(out=old[t][:], in_=page[t][:].indirect(n3_sb[:]), func=ACT.Copy)
+
+        def scalar_gather(dst, window, lst, width):
+            for h in range(2):
+                half = width // 2
+                nc.scalar.activation(
+                    out=dst[:, h * half : (h + 1) * half],
+                    in_=window[:].indirect(entries(lst, h * half, half)),
+                    func=ACT.Copy,
+                )
+
+        def square(t):
+            nc.scalar.activation(out=sq[t][:], in_=hy[t][:], func=ACT.Square, scale=2.0)
+
+        def denominator(t):
+            scalar_gather(sq_n1[t], sq[t], n1_sb, S)
+            den_ps[t] = bank(t)
+            for c in range(S // P):
+                cols = slice(c * P, (c + 1) * P)
+                for first, term in ((True, sq[t]), (False, sq_n1[t])):
+                    nc.tensor.matmul(
+                        out=den_ps[t][:, cols], lhsT=term[:, cols], rhs=ident[:], is_transpose=True, start=first, stop=not first
+                    )
+
+        def weigh_page_scalar(t):
+            nc.scalar.activation(out=z2_rows[:, t, :], in_=page[t][:], func=ACT.Copy, scale=gb_sb[:, t : t + 1])
+
+        def weigh_page_vector(t):
+            nc.vector.tensor_scalar(
+                out=z2_rows[:, t, :], in0=page[t][:], scalar1=gb_sb[:, t : t + 1], scalar2=None, op0=ALU.mult
+            )
+
+        def inverse_root(t):
+            nc.scalar.activation(
+                out=inv_t[t][:], in_=den_ps[t][:], func=ACT.Abs_reciprocal_sqrt, scale=0.25, bias=sixteenth[:]
+            )
+            inv_ps[t] = bank(4 + t)
+            for c in range(S // P):
+                cols = slice(c * P, (c + 1) * P)
+                nc.tensor.transpose(inv_ps[t][:, cols], inv_t[t][:, cols], ident[:])
+
+        def make_z(t):
+            scalar_gather(hy_n2[t], hy[t], n2_sb, S)
+            nc.vector.scalar_tensor_tensor(
+                out=z_rows[:, t, :], in0=hy_n2[t][:], scalar=ga_sb[:, t : t + 1], in1=inv_ps[t][:], op0=ALU.mult, op1=ALU.mult
+            )
+
+        z2_bf = {}
+        z2_codes = keep.tile([P, U], U32, align_bytes=64, name="z2_codes")
+        z2_scale = keep.tile([P, U], U8, align_bytes=64, name="z2_scale")
+        z_bf = keep.tile([P, PACK, P, PACK], BF16, align_bytes=64, name="z_bf")
+        z_codes = keep.tile([P, S], U32, align_bytes=64, name="z_codes")
+        z_scale = keep.tile([P, S], U8, align_bytes=64, name="z_scale")
+        z_src = z_rows[:].rearrange("p j (m i t) -> p t m j i", i=2, t=PACK)
+        s_sb = row_tiles("s", U, F32)
+        s_n4 = row_tiles("sn4", U, F32)
+        res = row_tiles("res", U, F32)
+        s_ps = {}
+
+        def slots(h):
+            return slice(h * HALF_U, (h + 1) * HALF_U)
+
+        def weave_z2(h, buffer):
+            z2_bf[h] = keep.tile([P, HALF_U, PACK], BF16, align_bytes=64, name=buffer)
+            nc.vector.tensor_copy(
+                out=z2_bf[h][:].rearrange("p (c i) j -> p c j i", i=4),
+                in_=z2_rows[:, :, slots(h)].rearrange("p j (c i) -> p c j i", i=4),
+            )
+
+        def quantize_z2(h):
+            nc.vector.quantize_mx(
+                out=z2_codes[:, slots(h)].bitcast(FP8X4),
+                scales=z2_scale[:, slots(h)],
+                in_=z2_bf[h][:].rearrange("p c j -> p (c j)"),
+            )
+
+        def deal_z(t, copy):
+            copy(out=z_bf[:, t].rearrange("p (m i) j -> p m j i", i=2), in_=z_src[:, t])
+
+        def quantize_z(t):
+            places = slice(t * P, (t + 1) * P)
+            nc.vector.quantize_mx(
+                out=z_codes[:, places].bitcast(FP8X4),
+                scales=z_scale[:, places],
+                in_=z_bf[:, t].rearrange("p m j -> p (m j)"),
+            )
+
+        def scores(t, h):
+            places = slice(t * P, (t + 1) * P)
+            s_ps[t, h] = bank(t + 4 * h)
+            nc.tensor.matmul_mx(
+                out=s_ps[t, h][:],
+                lhsT=z_codes[:, places].bitcast(FP8X4),
+                lhsT_scale=z_scale[:, places],
+                rhs=z2_codes[:, slots(h)].bitcast(FP8X4),
+                rhs_scale=z2_scale[:, slots(h)],
+                start=True,
+                stop=True,
+            )
+
+        def empty_scalar(t, h):
+            nc.scalar.activation(out=s_sb[t][:, slots(h)], in_=s_ps[t, h][:], func=ACT.Copy, scale=0.0625)
+
+        def empty_vector(t, h):
+            nc.vector.tensor_scalar(out=s_sb[t][:, slots(h)], in0=s_ps[t, h][:], scalar1=0.0625, scalar2=None, op0=ALU.mult)
+
+        def finish(t, widths):
+            start = 0
+            for width in widths:
+                cols = slice(start, start + width)
+                nc.scalar.activation(
+                    out=s_n4[t][:, cols], in_=s_sb[t][:].indirect(entries(n4_sb, start, width)), func=ACT.Copy
+                )
+                nc.vector.tensor_tensor(
+                    out=res[t][:, cols],
+                    in0=s_sb[t][:].indirect(entries(n5_sb, start, width)),
+                    in1=s_n4[t][:, cols],
+                    op=ALU.mult,
+                )
+                nc.sync.dma_start(out=out_rows[t][:, cols], in_=res[t][:, cols])
+                start = start + width
+
+        nc.vector.tensor_copy(out=old[0][:], in_=page[0][:].indirect(n3_sb[:]))
+        fetch_y(0)
+        write_page(0)
+        for t in range(1, PACK):
+            fetch_y(t)
+            fetch_old(t)
+            write_page(t)
+        for t in range(PACK):
+            square(t)
+        for t in range(PACK):
+            denominator(t)
+        weigh_page_scalar(0)
+        weigh_page_scalar(1)
+        weigh_page_vector(2)
+        weigh_page_vector(3)
+        for t in range(PACK):
+            inverse_root(t)
+        weave_z2(0, "z2_bf0")
+        weave_z2(1, "z2_bf1")
+        quantize_z2(0)
+        quantize_z2(1)
+        for t in range(PACK):
+            make_z(t)
+        deal_z(0, nc.vector.tensor_copy)
+        deal_z(1, nc.scalar.copy)
+        deal_z(2, nc.scalar.copy)
+        deal_z(3, nc.scalar.copy)
+        for t in range(PACK):
+            quantize_z(t)
+            scores(t, 0)
+            scores(t, 1)
+        empty_scalar(0, 0)
+        empty_vector(0, 1)
+        empty_vector(1, 0)
+        empty_vector(1, 1)
+        empty_vector(2, 0)
+        empty_vector(2, 1)
+        finish(0, (512, 512))
+        finish(1, (512, 512))
+        empty_scalar(3, 0)
+        empty_scalar(3, 1)
+        finish(2, (512, 512))
+        finish(3, (512, 256, 256))

@@ -74,15 +74,15 @@ def tile_picked_selfrmspagetprod_none_p_kernel(
         nc.sync.dma_start(out=n1_sb[:], in_=n1)
         nc.sync.dma_start(out=page[2][:], in_=mem_rows[2])
         nc.sync.dma_start(out=page[3][:], in_=mem_rows[3])
+        nc.sync.dma_start(out=gb_sb[:], in_=gb.rearrange("(p t) o -> p (t o)", t=PACK))
+        nc.sync.dma_start(out=ga_sb[:], in_=ga.rearrange("(p t) o -> p (t o)", t=PACK))
         nc.sync.dma_start(out=n2_sb[:], in_=n2)
         nc.sync.dma_start(out=n4_sb[:], in_=n4)
         nc.sync.dma_start(out=n5_sb[:], in_=n5)
-        nc.gpsimd.dma_start(out=gb_sb[:], in_=gb.rearrange("(p t) o -> p (t o)", t=PACK))
-        nc.gpsimd.dma_start(out=ga_sb[:], in_=ga.rearrange("(p t) o -> p (t o)", t=PACK))
         ident = keep.tile([P, P], F32, align_bytes=64, name="ident")
         make_identity(nc, ident[:])
-        sixteenth = keep.tile([P, 1], F32, name="sixteenth")
-        nc.gpsimd.memset(sixteenth[:], 0.0625)
+        quarter = keep.tile([P, 1], F32, name="quarter")
+        nc.gpsimd.memset(quarter[:], 0.25)
 
         w_bf = keep.tile([P, PACK, P, PACK], BF16, align_bytes=64, name="w_bf")
         w_dst = w_bf[:].rearrange("p t m j -> p m j t")
@@ -112,34 +112,37 @@ def tile_picked_selfrmspagetprod_none_p_kernel(
                 stop=True,
             )
 
-        hy = row_tiles("hy", S, F32)
-        th = row_tiles("th", S, F32)
-        old = row_tiles("old", S, F32)
-        diff = row_tiles("diff", S, F32)
-        step = row_tiles("step", S, F32)
-        sq = row_tiles("sq", S, F32)
+        def tile_f32(buffer):
+            return keep.tile([P, S], F32, name=buffer, align_bytes=64)
+
+        y = {}
+        gate = row_tiles("gate", S, F32)
+        old = {}
+        new = {}
+        sq = {}
         sq_n1 = row_tiles("sqn1", S, F32)
         inv_t = row_tiles("invT", S, F32)
-        hy_n2 = row_tiles("hyn2", S, F32)
-        z_rows = keep.tile([P, PACK, S], BF16, align_bytes=64, name="z_rows")
-        z2_rows = keep.tile([P, PACK, U], BF16, align_bytes=64, name="z2_rows")
+        y_n2 = row_tiles("yn2", S, F32)
         den_ps = {}
         inv_ps = {}
 
-        def fetch_y(t):
-            nc.scalar.activation(out=hy[t][:], in_=y_ps[t][:], func=ACT.Copy, scale=0.5)
-            nc.scalar.activation(out=th[t][:], in_=y_ps[t][:], func=ACT.Tanh, scale=0.5)
+        def sigmoid_y(t):
+            nc.scalar.activation(out=gate[t][:], in_=y_ps[t][:], func=ACT.Sigmoid)
 
-        def write_page(t):
-            nc.vector.scalar_tensor_tensor(
-                out=diff[t][:], in0=old[t][:], scalar=-0.5, in1=hy[t][:], op0=ALU.mult, op1=ALU.add
-            )
-            nc.vector.scalar_tensor_tensor(
-                out=step[t][:], in0=th[t][:], scalar=1.0, in1=diff[t][:], op0=ALU.add, op1=ALU.mult
-            )
-            nc.vector.tensor_tensor(out=page[t][:].indirect(n3_sb[:]), in0=step[t][:], in1=old[t][:], op=ALU.add)
+        def fetch_y(t, buffer, copy):
+            y[t] = tile_f32(buffer)
+            copy(out=y[t][:], in_=y_ps[t][:])
+
+        def write_page(t, engine, y_t):
+            step = tile_f32("step")
+            engine.tensor_tensor(out=step[:], in0=y_t[:], in1=old[t][:], op=ALU.subtract)
+            engine.tensor_tensor(out=step[:], in0=step[:], in1=gate[t][:], op=ALU.mult)
+            new[t] = tile_f32("new%d" % t)
+            engine.tensor_tensor(out=new[t][:], in0=step[:], in1=old[t][:], op=ALU.add)
+            nc.vector.tensor_copy(out=page[t][:].indirect(n3_sb[:]), in_=new[t][:])
 
         def fetch_old(t):
+            old[t] = tile_f32("old%d" % t)
             nc.scalar.activation(out=old[t][:], in_=page[t][:].indirect(n3_sb[:]), func=ACT.Copy)
 
         def scalar_gather(dst, window, lst, width):
@@ -151,8 +154,13 @@ def tile_picked_selfrmspagetprod_none_p_kernel(
                     func=ACT.Copy,
                 )
 
-        def square(t):
-            nc.scalar.activation(out=sq[t][:], in_=hy[t][:], func=ACT.Square, scale=2.0)
+        def square_scalar(t):
+            sq[t] = tile_f32("sq%d" % t)
+            nc.scalar.activation(out=sq[t][:], in_=y_ps[t][:], func=ACT.Square)
+
+        def square_vector(t, buffer):
+            sq[t] = tile_f32(buffer)
+            nc.vector.tensor_tensor(out=sq[t][:], in0=y_ps[t][:], in1=y[t][:], op=ALU.mult)
 
         def denominator(t):
             scalar_gather(sq_n1[t], sq[t], n1_sb, S)
@@ -172,9 +180,14 @@ def tile_picked_selfrmspagetprod_none_p_kernel(
                 out=z2_rows[:, t, :], in0=page[t][:], scalar1=gb_sb[:, t : t + 1], scalar2=None, op0=ALU.mult
             )
 
+        def weigh_page_gpsimd(t):
+            nc.gpsimd.tensor_scalar(
+                out=z2_rows[:, t, :], in0=page[t][:], scalar1=gb_sb[:, t : t + 1], scalar2=0.0, op0=ALU.mult, op1=ALU.add
+            )
+
         def inverse_root(t):
             nc.scalar.activation(
-                out=inv_t[t][:], in_=den_ps[t][:], func=ACT.Abs_reciprocal_sqrt, scale=0.25, bias=sixteenth[:]
+                out=inv_t[t][:], in_=den_ps[t][:], func=ACT.Abs_reciprocal_sqrt, bias=quarter[:]
             )
             inv_ps[t] = bank(4 + t)
             for c in range(S // P):
@@ -182,9 +195,9 @@ def tile_picked_selfrmspagetprod_none_p_kernel(
                 nc.tensor.transpose(inv_ps[t][:, cols], inv_t[t][:, cols], ident[:])
 
         def make_z(t):
-            scalar_gather(hy_n2[t], hy[t], n2_sb, S)
+            scalar_gather(y_n2[t], y[t], n2_sb, S)
             nc.vector.scalar_tensor_tensor(
-                out=z_rows[:, t, :], in0=hy_n2[t][:], scalar=ga_sb[:, t : t + 1], in1=inv_ps[t][:], op0=ALU.mult, op1=ALU.mult
+                out=z_rows[:, t, :], in0=y_n2[t][:], scalar=ga_sb[:, t : t + 1], in1=inv_ps[t][:], op0=ALU.mult, op1=ALU.mult
             )
 
         z2_bf = {}
@@ -193,7 +206,6 @@ def tile_picked_selfrmspagetprod_none_p_kernel(
         z_bf = keep.tile([P, PACK, P, PACK], BF16, align_bytes=64, name="z_bf")
         z_codes = keep.tile([P, S], U32, align_bytes=64, name="z_codes")
         z_scale = keep.tile([P, S], U8, align_bytes=64, name="z_scale")
-        z_src = z_rows[:].rearrange("p j (m i t) -> p t m j i", i=2, t=PACK)
         s_sb = row_tiles("s", U, F32)
         s_n4 = row_tiles("sn4", U, F32)
         res = row_tiles("res", U, F32)
@@ -202,18 +214,36 @@ def tile_picked_selfrmspagetprod_none_p_kernel(
         def slots(h):
             return slice(h * HALF_U, (h + 1) * HALF_U)
 
-        def weave_z2(h, buffer):
-            z2_bf[h] = keep.tile([P, HALF_U, PACK], BF16, align_bytes=64, name=buffer)
+        def weave_z2_vector(start, width, buffer):
+            z2_bf[start] = keep.tile([P, width, PACK], BF16, align_bytes=64, name=buffer)
             nc.vector.tensor_copy(
-                out=z2_bf[h][:].rearrange("p (c i) j -> p c j i", i=4),
-                in_=z2_rows[:, :, slots(h)].rearrange("p j (c i) -> p c j i", i=4),
+                out=z2_bf[start][:].rearrange("p (c i) j -> p c j i", i=4),
+                in_=z2_rows[:, :, start : start + width].rearrange("p j (c i) -> p c j i", i=4),
             )
 
-        def quantize_z2(h):
+        def weave_z2_scalar(start, width, buffer):
+            z2_bf[start] = keep.tile([P, width, PACK], BF16, align_bytes=64, name=buffer)
+            nc.scalar.copy(
+                out=z2_bf[start][:].rearrange("p (c i) j -> p c j i", i=4),
+                in_=z2_rows[:, :, start : start + width].rearrange("p j (c i) -> p c j i", i=4),
+            )
+
+        def weave_z2_gpsimd(start, width, buffer):
+            z2_bf[start] = keep.tile([P, width, PACK], BF16, align_bytes=64, name=buffer)
+            nc.gpsimd.tensor_scalar(
+                out=z2_bf[start][:],
+                in0=z2_rows[:, :, start : start + width].rearrange("p j c -> p c j"),
+                scalar1=1.0,
+                scalar2=0.0,
+                op0=ALU.mult,
+                op1=ALU.add,
+            )
+
+        def quantize_z2(start, width):
             nc.vector.quantize_mx(
-                out=z2_codes[:, slots(h)].bitcast(FP8X4),
-                scales=z2_scale[:, slots(h)],
-                in_=z2_bf[h][:].rearrange("p c j -> p (c j)"),
+                out=z2_codes[:, start : start + width].bitcast(FP8X4),
+                scales=z2_scale[:, start : start + width],
+                in_=z2_bf[start][:].rearrange("p c j -> p (c j)"),
             )
 
         def deal_z(t, copy):
@@ -262,34 +292,43 @@ def tile_picked_selfrmspagetprod_none_p_kernel(
                 nc.sync.dma_start(out=out_rows[t][:, cols], in_=res[t][:, cols])
                 start = start + width
 
+        old[0] = tile_f32("w_bf")
         nc.vector.tensor_copy(out=old[0][:], in_=page[0][:].indirect(n3_sb[:]))
-        fetch_y(0)
-        write_page(0)
+        sigmoid_y(0)
+        write_page(0, nc.vector, y_ps[0])
         for t in range(1, PACK):
-            fetch_y(t)
+            fetch_y(t, "y%d" % t, nc.scalar.copy)
+            sigmoid_y(t)
             fetch_old(t)
-            write_page(t)
-        for t in range(PACK):
-            square(t)
+            write_page(t, nc.gpsimd, y[t])
+        fetch_y(0, "new0", nc.vector.tensor_copy)
+        square_scalar(0)
+        square_scalar(1)
+        square_vector(2, "new1")
+        square_vector(3, "new2")
         for t in range(PACK):
             denominator(t)
-        weigh_page_scalar(0)
-        weigh_page_scalar(1)
-        weigh_page_vector(2)
+        z2_rows = keep.tile([P, PACK, U], BF16, align_bytes=64, name="step")
+        weigh_page_gpsimd(0)
+        weigh_page_gpsimd(1)
+        weigh_page_gpsimd(2)
         weigh_page_vector(3)
         for t in range(PACK):
             inverse_root(t)
-        weave_z2(0, "z2_bf0")
-        weave_z2(1, "z2_bf1")
-        quantize_z2(0)
-        quantize_z2(1)
+        weave_z2_vector(0, 256, "z2_bf0")
+        weave_z2_vector(256, 256, "z2_bf1")
+        quantize_z2(0, 256)
+        quantize_z2(256, 256)
+        weave_z2_gpsimd(512, 384, "z2_bf1")
+        weave_z2_scalar(896, 128, "z2_bf3")
+        z_rows = keep.tile([P, PACK, S], BF16, align_bytes=64, name="z2_bf0")
+        z_src = z_rows[:].rearrange("p j (m i t) -> p t m j i", i=2, t=PACK)
         for t in range(PACK):
             make_z(t)
-        deal_z(0, nc.vector.tensor_copy)
-        deal_z(1, nc.scalar.copy)
-        deal_z(2, nc.scalar.copy)
-        deal_z(3, nc.scalar.copy)
+        quantize_z2(896, 128)
+        quantize_z2(512, 384)
         for t in range(PACK):
+            deal_z(t, nc.vector.tensor_copy if t % 2 else nc.scalar.copy)
             quantize_z(t)
             scores(t, 0)
             scores(t, 1)

@@ -133,10 +133,11 @@ def tile_picked_selfrmspagetprod_none_p_kernel(
             y[t] = tile_f32(buffer)
             copy(out=y[t][:], in_=y_ps[t][:])
 
-        def write_page(t, engine, y_t):
+        def write_page(t, engine):
+            diff = tile_f32("diff%d" % t)
+            nc.vector.tensor_tensor(out=diff[:], in0=y_ps[t][:], in1=old[t][:], op=ALU.subtract)
             step = tile_f32("step")
-            engine.tensor_tensor(out=step[:], in0=y_t[:], in1=old[t][:], op=ALU.subtract)
-            engine.tensor_tensor(out=step[:], in0=step[:], in1=gate[t][:], op=ALU.mult)
+            engine.tensor_tensor(out=step[:], in0=diff[:], in1=gate[t][:], op=ALU.mult)
             new[t] = tile_f32("new%d" % t)
             engine.tensor_tensor(out=new[t][:], in0=step[:], in1=old[t][:], op=ALU.add)
             nc.vector.tensor_copy(out=page[t][:].indirect(n3_sb[:]), in_=new[t][:])
@@ -156,7 +157,11 @@ def tile_picked_selfrmspagetprod_none_p_kernel(
 
         def square_scalar(t):
             sq[t] = tile_f32("sq%d" % t)
-            nc.scalar.activation(out=sq[t][:], in_=y_ps[t][:], func=ACT.Square)
+            nc.scalar.activation(out=sq[t][:], in_=y[t][:], func=ACT.Square)
+
+        def square_gpsimd(t, buffer):
+            sq[t] = tile_f32(buffer)
+            nc.gpsimd.tensor_tensor(out=sq[t][:], in0=y[t][:], in1=y[t][:], op=ALU.mult)
 
         def square_vector(t, buffer):
             sq[t] = tile_f32(buffer)
@@ -295,17 +300,18 @@ def tile_picked_selfrmspagetprod_none_p_kernel(
         old[0] = tile_f32("w_bf")
         nc.vector.tensor_copy(out=old[0][:], in_=page[0][:].indirect(n3_sb[:]))
         sigmoid_y(0)
-        write_page(0, nc.vector, y_ps[0])
+        write_page(0, nc.vector)
         for t in range(1, PACK):
-            fetch_y(t, "y%d" % t, nc.scalar.copy)
             sigmoid_y(t)
+            fetch_y(t, "y%d" % t, nc.scalar.copy)
             fetch_old(t)
-            write_page(t, nc.gpsimd, y[t])
-        fetch_y(0, "new0", nc.vector.tensor_copy)
+            if t == 2:
+                square_gpsimd(t, "old1")
+            write_page(t, nc.gpsimd)
+        fetch_y(0, "y0", nc.scalar.copy)
         square_scalar(0)
         square_scalar(1)
-        square_vector(2, "new1")
-        square_vector(3, "new2")
+        square_vector(3, "sq3")
         for t in range(PACK):
             denominator(t)
         z2_rows = keep.tile([P, PACK, U], BF16, align_bytes=64, name="step")
@@ -316,17 +322,15 @@ def tile_picked_selfrmspagetprod_none_p_kernel(
         for t in range(PACK):
             inverse_root(t)
         weave_z2_vector(0, 256, "z2_bf0")
-        weave_z2_vector(256, 256, "z2_bf1")
+        weave_z2_vector(256, 384, "z2_bf1")
         quantize_z2(0, 256)
-        quantize_z2(256, 256)
-        weave_z2_gpsimd(512, 384, "z2_bf1")
-        weave_z2_scalar(896, 128, "z2_bf3")
+        quantize_z2(256, 384)
+        weave_z2_gpsimd(640, 384, "z2_bf1")
         z_rows = keep.tile([P, PACK, S], BF16, align_bytes=64, name="z2_bf0")
         z_src = z_rows[:].rearrange("p j (m i t) -> p t m j i", i=2, t=PACK)
         for t in range(PACK):
             make_z(t)
-        quantize_z2(896, 128)
-        quantize_z2(512, 384)
+        quantize_z2(640, 384)
         for t in range(PACK):
             deal_z(t, nc.vector.tensor_copy if t % 2 else nc.scalar.copy)
             quantize_z(t)

@@ -133,13 +133,18 @@ def tile_picked_selfrmspagetprod_none_p_kernel(
             y[t] = tile_f32(buffer)
             copy(out=y[t][:], in_=y_ps[t][:])
 
-        def write_page(t, engine):
-            diff = tile_f32("diff%d" % t)
-            nc.vector.tensor_tensor(out=diff[:], in0=y_ps[t][:], in1=old[t][:], op=ALU.subtract)
+        diff = row_tiles("diff", S, F32)
+
+        def difference(t, cols):
+            nc.vector.tensor_tensor(out=diff[t][:, cols], in0=y_ps[t][:, cols], in1=old[t][:, cols], op=ALU.subtract)
+
+        def write_page(t, engine, pieces):
             step = tile_f32("step")
-            engine.tensor_tensor(out=step[:], in0=diff[:], in1=gate[t][:], op=ALU.mult)
             new[t] = tile_f32("new%d" % t)
-            engine.tensor_tensor(out=new[t][:], in0=step[:], in1=old[t][:], op=ALU.add)
+            for cols in pieces:
+                engine.tensor_tensor(out=step[:, cols], in0=diff[t][:, cols], in1=gate[t][:, cols], op=ALU.mult)
+            for cols in pieces:
+                engine.tensor_tensor(out=new[t][:, cols], in0=step[:, cols], in1=old[t][:, cols], op=ALU.add)
             nc.vector.tensor_copy(out=page[t][:].indirect(n3_sb[:]), in_=new[t][:])
 
         def fetch_old(t):
@@ -180,9 +185,9 @@ def tile_picked_selfrmspagetprod_none_p_kernel(
         def weigh_page_scalar(t):
             nc.scalar.activation(out=z2_rows[:, t, :], in_=page[t][:], func=ACT.Copy, scale=gb_sb[:, t : t + 1])
 
-        def weigh_page_vector(t):
+        def weigh_page_vector(t, cols):
             nc.vector.tensor_scalar(
-                out=z2_rows[:, t, :], in0=page[t][:], scalar1=gb_sb[:, t : t + 1], scalar2=None, op0=ALU.mult
+                out=z2_rows[:, t, cols], in0=page[t][:, cols], scalar1=gb_sb[:, t : t + 1], scalar2=None, op0=ALU.mult
             )
 
         def weigh_page_gpsimd(t):
@@ -262,24 +267,28 @@ def tile_picked_selfrmspagetprod_none_p_kernel(
                 in_=z_bf[:, t].rearrange("p m j -> p (m j)"),
             )
 
-        def scores(t, h):
+        def scores(t, start, width, b):
             places = slice(t * P, (t + 1) * P)
-            s_ps[t, h] = bank(t + 4 * h)
+            s_ps[t, start] = bank(b)
             nc.tensor.matmul_mx(
-                out=s_ps[t, h][:],
+                out=s_ps[t, start][:, 0:width],
                 lhsT=z_codes[:, places].bitcast(FP8X4),
                 lhsT_scale=z_scale[:, places],
-                rhs=z2_codes[:, slots(h)].bitcast(FP8X4),
-                rhs_scale=z2_scale[:, slots(h)],
+                rhs=z2_codes[:, start : start + width].bitcast(FP8X4),
+                rhs_scale=z2_scale[:, start : start + width],
                 start=True,
                 stop=True,
             )
 
-        def empty_scalar(t, h):
-            nc.scalar.activation(out=s_sb[t][:, slots(h)], in_=s_ps[t, h][:], func=ACT.Copy, scale=0.0625)
+        def empty_scalar(t, start, lo, hi):
+            nc.scalar.activation(
+                out=s_sb[t][:, start + lo : start + hi], in_=s_ps[t, start][:, lo:hi], func=ACT.Copy, scale=0.0625
+            )
 
-        def empty_vector(t, h):
-            nc.vector.tensor_scalar(out=s_sb[t][:, slots(h)], in0=s_ps[t, h][:], scalar1=0.0625, scalar2=None, op0=ALU.mult)
+        def empty_vector(t, start, lo, hi):
+            nc.vector.tensor_scalar(
+                out=s_sb[t][:, start + lo : start + hi], in0=s_ps[t, start][:, lo:hi], scalar1=0.0625, scalar2=None, op0=ALU.mult
+            )
 
         def finish(t, widths):
             start = 0
@@ -297,18 +306,29 @@ def tile_picked_selfrmspagetprod_none_p_kernel(
                 nc.sync.dma_start(out=out_rows[t][:, cols], in_=res[t][:, cols])
                 start = start + width
 
-        old[0] = tile_f32("w_bf")
-        nc.vector.tensor_copy(out=old[0][:], in_=page[0][:].indirect(n3_sb[:]))
+        halves = (slice(0, HALF_S), slice(HALF_S, S))
+        whole = (slice(0, S),)
+        old[0] = tile_f32("w_raw1")
+        for h in range(2):
+            nc.vector.tensor_copy(out=old[0][:, halves[h]], in_=page[0][:].indirect(entries(n3_sb, h * HALF_S, HALF_S)))
         sigmoid_y(0)
-        write_page(0, nc.vector)
-        for t in range(1, PACK):
+        for cols in halves:
+            difference(0, cols)
+        write_page(0, nc.vector, halves)
+        fetch_old(1)
+        sigmoid_y(1)
+        difference(1, whole[0])
+        write_page(1, nc.gpsimd, whole)
+        for t in range(2, PACK):
             sigmoid_y(t)
             fetch_y(t, "y%d" % t, nc.scalar.copy)
             fetch_old(t)
+            difference(t, whole[0])
             if t == 2:
                 square_gpsimd(t, "old1")
-            write_page(t, nc.gpsimd)
-        fetch_y(0, "y0", nc.scalar.copy)
+            write_page(t, nc.gpsimd, whole)
+        for t in range(2):
+            fetch_y(t, "y%d" % t, nc.scalar.copy)
         square_scalar(0)
         square_scalar(1)
         square_vector(3, "sq3")
@@ -318,7 +338,8 @@ def tile_picked_selfrmspagetprod_none_p_kernel(
         weigh_page_gpsimd(0)
         weigh_page_gpsimd(1)
         weigh_page_gpsimd(2)
-        weigh_page_vector(3)
+        weigh_page_vector(3, slice(0, 640))
+        weigh_page_vector(3, slice(640, U))
         for t in range(PACK):
             inverse_root(t)
         weave_z2_vector(0, 256, "z2_bf0")
@@ -331,20 +352,24 @@ def tile_picked_selfrmspagetprod_none_p_kernel(
         for t in range(PACK):
             make_z(t)
         quantize_z2(640, 384)
-        for t in range(PACK):
+        deal_z(0, nc.scalar.copy)
+        quantize_z(0)
+        for q, b in enumerate((0, 4, 3, 7)):
+            scores(0, 256 * q, 256, b)
+        for q in range(4):
+            (empty_vector if q % 2 else empty_scalar)(0, 256 * q, 0, 256)
+        for t in range(1, PACK):
             deal_z(t, nc.vector.tensor_copy if t % 2 else nc.scalar.copy)
             quantize_z(t)
-            scores(t, 0)
-            scores(t, 1)
-        empty_scalar(0, 0)
-        empty_vector(0, 1)
-        empty_vector(1, 0)
-        empty_vector(1, 1)
-        empty_vector(2, 0)
-        empty_vector(2, 1)
+            scores(t, 0, 512, t)
+            scores(t, 512, 512, 4 + t)
+        empty_vector(1, 0, 0, 512)
+        empty_vector(1, 512, 0, 512)
+        empty_vector(2, 0, 0, 512)
+        empty_vector(2, 512, 0, 512)
         finish(0, (512, 512))
         finish(1, (512, 512))
-        empty_scalar(3, 0)
-        empty_scalar(3, 1)
+        empty_scalar(3, 0, 0, 512)
+        empty_scalar(3, 512, 0, 512)
         finish(2, (512, 512))
         finish(3, (512, 256, 256))

@@ -18,10 +18,16 @@ ALU = mybir.AluOpType
 
 P = 128
 PACK = 4
-W_VECTOR = 44
+BANK = 512
+LIST_COLUMN = 16
+QUADRANTS = 4
 HALF_H = H // 2
 HALF_S = S // 2
-HALF_U = U // 2
+QUARTER_U = U // 4
+W_VECTOR = 44
+Z2_PIECES = ((0, 256), (256, 384), (640, 384))
+OUT_PIECES = (512, 512)
+LAST_OUT_PIECES = (512, 256, 256)
 
 
 def tile_picked_selfrmspagetprod_none_p_kernel(
@@ -33,35 +39,38 @@ def tile_picked_selfrmspagetprod_none_p_kernel(
         keep = ctx.enter_context(tc.tile_pool(name="keep", bufs=1))
         psum = ctx.enter_context(tc.psum_pool(name="psum", bufs=1))
 
-        def entries(lst, start, count):
-            return lst[:, start // 16 : (start + count) // 16]
+        def sbuf(name, shape, dtype, tag=""):
+            return keep.tile([P] + shape, dtype, name=name, tag=tag or name, align_bytes=64)
 
-        def row_tiles(name, width, dtype):
-            return [keep.tile([P, width], dtype, name="%s%d" % (name, t), align_bytes=64) for t in range(PACK)]
+        def row_tiles(name, width):
+            return [sbuf("%s%d" % (name, t), [width], F32) for t in range(PACK)]
 
         def bank(b):
-            return psum.tile([P, 512], F32, name="bank%d" % b)
+            return psum.tile([P, BANK], F32, name="bank%d" % b)
 
-        offs_sb = lists.tile([P, S // 16], U16, name="offs_sb")
-        n1_sb = lists.tile([P, S // 16], U16, name="n1_sb")
-        n2_sb = lists.tile([P, S // 16], U16, name="n2_sb")
-        n3_sb = lists.tile([P, S // 16], U16, name="n3_sb")
-        n4_sb = lists.tile([P, U // 16], U16, name="n4_sb")
-        n5_sb = lists.tile([P, U // 16], U16, name="n5_sb")
+        def entries(list_tile, start, count):
+            return list_tile[:, start // LIST_COLUMN : (start + count) // LIST_COLUMN]
 
-        xw_all = keep.tile([P, T], U32, align_bytes=64, name="xw_all")
-        xs_all = keep.tile([P, T], U8, align_bytes=64, name="xs_all")
-        w_raw = [keep.tile([P, PACK, HALF_H], F32, align_bytes=64, name="w_raw%d" % h) for h in range(2)]
-        ga_sb = keep.tile([P, PACK], F32, name="ga_sb")
-        gb_sb = keep.tile([P, PACK], F32, name="gb_sb")
-        page = row_tiles("page", U, F32)
+        offs_sb = lists.tile([P, S // LIST_COLUMN], U16)
+        n1_sb = lists.tile([P, S // LIST_COLUMN], U16)
+        n2_sb = lists.tile([P, S // LIST_COLUMN], U16)
+        n3_sb = lists.tile([P, S // LIST_COLUMN], U16)
+        n4_sb = lists.tile([P, U // LIST_COLUMN], U16)
+        n5_sb = lists.tile([P, U // LIST_COLUMN], U16)
+
+        xw_all = sbuf("xw_all", [T], U32)
+        xs_all = sbuf("xs_all", [T], U8)
+        w_raw = [sbuf("w_raw%d" % h, [PACK, HALF_H], F32) for h in range(2)]
+        ga_sb = keep.tile([P, PACK], F32)
+        gb_sb = keep.tile([P, PACK], F32)
+        page = row_tiles("page", U)
         mem_rows = mem.rearrange("(p t) w -> t p w", t=PACK)
         out_rows = out.rearrange("(p t) w -> t p w", t=PACK)
 
         nc.vector.memset(xs_all[:].bitcast(I32), 0)
         nc.sync.dma_start(out=offs_sb[:], in_=offs)
         nc.sync.dma_start(out=xw_all[:].bitcast(I32), in_=x_words[0].rearrange("p n r -> p (n r)").bitcast(I32))
-        for q in range(4):
+        for q in range(QUADRANTS):
             nc.sync.dma_start(
                 out=xs_all[32 * q : 32 * q + 4, :].bitcast(I32), in_=x_scales[0, 4 * q : 4 * q + 4, :].bitcast(I32)
             )
@@ -79,297 +88,273 @@ def tile_picked_selfrmspagetprod_none_p_kernel(
         nc.sync.dma_start(out=n2_sb[:], in_=n2)
         nc.sync.dma_start(out=n4_sb[:], in_=n4)
         nc.sync.dma_start(out=n5_sb[:], in_=n5)
-        ident = keep.tile([P, P], F32, align_bytes=64, name="ident")
+        ident = sbuf("ident", [P], F32)
         make_identity(nc, ident[:])
-        quarter = keep.tile([P, 1], F32, name="quarter")
-        nc.gpsimd.memset(quarter[:], 0.25)
+        root_bias = keep.tile([P, 1], F32)
+        nc.gpsimd.memset(root_bias[:], 0.25)
 
-        w_bf = keep.tile([P, PACK, P, PACK], BF16, align_bytes=64, name="w_bf")
+        w_bf = sbuf("w_bf", [PACK, P, PACK], BF16)
         w_dst = w_bf[:].rearrange("p t m j -> p m j t")
         w_src = [w_raw[h][:].rearrange("p j (m t) -> p m j t", t=PACK) for h in range(2)]
-        xw = keep.tile([P, S], U32, align_bytes=64, name="xw")
-        xs = keep.tile([P, S], U8, align_bytes=64, name="xs")
+        half_m = P // 2
+        xw = sbuf("xw", [S], U32)
+        xs = sbuf("xs", [S], U8)
         nc.vector.tensor_copy(out=xw[:], in_=xw_all[:].indirect(offs_sb[:]))
         nc.vector.tensor_copy(out=xs[:], in_=xs_all[:].indirect(offs_sb[:]))
-        nc.scalar.copy(out=w_dst[:, 0:64], in_=w_src[0])
-        nc.vector.tensor_copy(out=w_dst[:, 64 : 64 + W_VECTOR], in_=w_src[1][:, 0:W_VECTOR])
-        nc.scalar.copy(out=w_dst[:, 64 + W_VECTOR : P], in_=w_src[1][:, W_VECTOR:64])
-        w_codes = keep.tile([P, H], U32, align_bytes=64, name="w_codes")
-        w_scale = keep.tile([P, H], U8, align_bytes=64, name="w_scale")
-        y_ps = [bank(4 + t) for t in range(PACK)]
+        nc.scalar.copy(out=w_dst[:, 0:half_m], in_=w_src[0])
+        nc.vector.tensor_copy(out=w_dst[:, half_m : half_m + W_VECTOR], in_=w_src[1][:, 0:W_VECTOR])
+        nc.scalar.copy(out=w_dst[:, half_m + W_VECTOR : P], in_=w_src[1][:, W_VECTOR:half_m])
+        w_codes = sbuf("w_codes", [H], U32)
+        w_scale = sbuf("w_scale", [H], U8)
+        y_ps = [bank(PACK + t) for t in range(PACK)]
         for t in range(PACK):
-            feats = slice(t * P, (t + 1) * P)
+            features = slice(t * P, (t + 1) * P)
             nc.vector.quantize_mx(
-                out=w_codes[:, feats].bitcast(FP8X4), scales=w_scale[:, feats], in_=w_bf[:, t].rearrange("p m j -> p (m j)")
+                out=w_codes[:, features].bitcast(FP8X4),
+                scales=w_scale[:, features],
+                in_=w_bf[:, t].rearrange("p m j -> p (m j)"),
             )
             nc.tensor.matmul_mx(
                 out=y_ps[t][:],
-                lhsT=w_codes[:, feats].bitcast(FP8X4),
-                lhsT_scale=w_scale[:, feats],
+                lhsT=w_codes[:, features].bitcast(FP8X4),
+                lhsT_scale=w_scale[:, features],
                 rhs=xw[:].bitcast(FP8X4),
                 rhs_scale=xs[:],
                 start=True,
                 stop=True,
             )
 
-        def tile_f32(buffer):
-            return keep.tile([P, S], F32, name=buffer, align_bytes=64)
-
-        y = {}
-        gate = row_tiles("gate", S, F32)
+        y = row_tiles("y", S)
+        gate = row_tiles("gate", S)
+        diff = row_tiles("diff", S)
+        new = row_tiles("new", S)
         old = {}
-        new = {}
         sq = {}
-        sq_n1 = row_tiles("sqn1", S, F32)
-        inv_t = row_tiles("invT", S, F32)
-        y_n2 = row_tiles("yn2", S, F32)
-        den_ps = {}
-        inv_ps = {}
+        halves = [slice(h * HALF_S, (h + 1) * HALF_S) for h in range(2)]
+        whole = [slice(0, S)]
 
         def sigmoid_y(t):
             nc.scalar.activation(out=gate[t][:], in_=y_ps[t][:], func=ACT.Sigmoid)
 
-        def fetch_y(t, buffer, copy):
-            y[t] = tile_f32(buffer)
-            copy(out=y[t][:], in_=y_ps[t][:])
+        def copy_y(t):
+            nc.scalar.copy(out=y[t][:], in_=y_ps[t][:])
 
-        diff = row_tiles("diff", S, F32)
+        def fetch_old(t):
+            old[t] = sbuf("old%d" % t, [S], F32)
+            nc.scalar.activation(out=old[t][:], in_=page[t][:].indirect(n3_sb[:]), func=ACT.Copy)
 
-        def difference(t, cols):
-            nc.vector.tensor_tensor(out=diff[t][:, cols], in0=y_ps[t][:, cols], in1=old[t][:, cols], op=ALU.subtract)
+        def difference(t, pieces):
+            for cols in pieces:
+                nc.vector.tensor_tensor(
+                    out=diff[t][:, cols], in0=y_ps[t][:, cols], in1=old[t][:, cols], op=ALU.subtract
+                )
 
         def write_page(t, engine, pieces):
-            step = tile_f32("step")
-            new[t] = tile_f32("new%d" % t)
+            step = sbuf("step%d" % t, [S], F32, tag="step")
             for cols in pieces:
                 engine.tensor_tensor(out=step[:, cols], in0=diff[t][:, cols], in1=gate[t][:, cols], op=ALU.mult)
             for cols in pieces:
                 engine.tensor_tensor(out=new[t][:, cols], in0=step[:, cols], in1=old[t][:, cols], op=ALU.add)
             nc.vector.tensor_copy(out=page[t][:].indirect(n3_sb[:]), in_=new[t][:])
 
-        def fetch_old(t):
-            old[t] = tile_f32("old%d" % t)
-            nc.scalar.activation(out=old[t][:], in_=page[t][:].indirect(n3_sb[:]), func=ACT.Copy)
+        old[0] = sbuf("old0", [S], F32, tag="w_raw1")
+        for h in range(2):
+            nc.vector.tensor_copy(
+                out=old[0][:, halves[h]], in_=page[0][:].indirect(entries(n3_sb, h * HALF_S, HALF_S))
+            )
+        sigmoid_y(0)
+        difference(0, halves)
+        write_page(0, nc.vector, halves)
+        fetch_old(1)
+        sigmoid_y(1)
+        difference(1, whole)
+        write_page(1, nc.gpsimd, whole)
+        sigmoid_y(2)
+        copy_y(2)
+        fetch_old(2)
+        difference(2, whole)
+        sq[2] = sbuf("sq2", [S], F32, tag="old1")
+        nc.gpsimd.tensor_tensor(out=sq[2][:], in0=y[2][:], in1=y[2][:], op=ALU.mult)
+        write_page(2, nc.gpsimd, whole)
+        sigmoid_y(3)
+        copy_y(3)
+        fetch_old(3)
+        difference(3, whole)
+        write_page(3, nc.gpsimd, whole)
 
-        def scalar_gather(dst, window, lst, width):
+        for t in range(2):
+            copy_y(t)
+        for t in range(2):
+            sq[t] = sbuf("sq%d" % t, [S], F32)
+            nc.scalar.activation(out=sq[t][:], in_=y[t][:], func=ACT.Square)
+        sq[3] = sbuf("sq3", [S], F32)
+        nc.vector.tensor_tensor(out=sq[3][:], in0=y_ps[3][:], in1=y[3][:], op=ALU.mult)
+
+        def gather_places(dst, window, list_tile):
             for h in range(2):
-                half = width // 2
                 nc.scalar.activation(
-                    out=dst[:, h * half : (h + 1) * half],
-                    in_=window[:].indirect(entries(lst, h * half, half)),
-                    func=ACT.Copy,
+                    out=dst[:, halves[h]], in_=window[:].indirect(entries(list_tile, h * HALF_S, HALF_S)), func=ACT.Copy
                 )
 
-        def square_scalar(t):
-            sq[t] = tile_f32("sq%d" % t)
-            nc.scalar.activation(out=sq[t][:], in_=y[t][:], func=ACT.Square)
-
-        def square_gpsimd(t, buffer):
-            sq[t] = tile_f32(buffer)
-            nc.gpsimd.tensor_tensor(out=sq[t][:], in0=y[t][:], in1=y[t][:], op=ALU.mult)
-
-        def square_vector(t, buffer):
-            sq[t] = tile_f32(buffer)
-            nc.vector.tensor_tensor(out=sq[t][:], in0=y_ps[t][:], in1=y[t][:], op=ALU.mult)
-
-        def denominator(t):
-            scalar_gather(sq_n1[t], sq[t], n1_sb, S)
-            den_ps[t] = bank(t)
-            for c in range(S // P):
-                cols = slice(c * P, (c + 1) * P)
+        sq_n1 = row_tiles("sq_n1_", S)
+        blocks = [slice(c * P, (c + 1) * P) for c in range(S // P)]
+        sum_ps = []
+        for t in range(PACK):
+            gather_places(sq_n1[t], sq[t], n1_sb)
+            sum_ps.append(bank(t))
+            for cols in blocks:
                 for first, term in ((True, sq[t]), (False, sq_n1[t])):
                     nc.tensor.matmul(
-                        out=den_ps[t][:, cols], lhsT=term[:, cols], rhs=ident[:], is_transpose=True, start=first, stop=not first
+                        out=sum_ps[t][:, cols],
+                        lhsT=term[:, cols],
+                        rhs=ident[:],
+                        is_transpose=True,
+                        start=first,
+                        stop=not first,
                     )
 
-        def weigh_page_scalar(t):
-            nc.scalar.activation(out=z2_rows[:, t, :], in_=page[t][:], func=ACT.Copy, scale=gb_sb[:, t : t + 1])
-
-        def weigh_page_vector(t, cols):
-            nc.vector.tensor_scalar(
-                out=z2_rows[:, t, cols], in0=page[t][:, cols], scalar1=gb_sb[:, t : t + 1], scalar2=None, op0=ALU.mult
-            )
-
-        def weigh_page_gpsimd(t):
+        z2_rows = sbuf("z2_rows", [PACK, U], BF16, tag="step")
+        for t in range(PACK - 1):
             nc.gpsimd.tensor_scalar(
                 out=z2_rows[:, t, :], in0=page[t][:], scalar1=gb_sb[:, t : t + 1], scalar2=0.0, op0=ALU.mult, op1=ALU.add
             )
-
-        def inverse_root(t):
-            nc.scalar.activation(
-                out=inv_t[t][:], in_=den_ps[t][:], func=ACT.Abs_reciprocal_sqrt, bias=quarter[:]
+        last = PACK - 1
+        gpsimd_start, gpsimd_width = Z2_PIECES[-1]
+        for cols in (slice(0, gpsimd_start), slice(gpsimd_start, U)):
+            nc.vector.tensor_scalar(
+                out=z2_rows[:, last, cols],
+                in0=page[last][:, cols],
+                scalar1=gb_sb[:, last : last + 1],
+                scalar2=None,
+                op0=ALU.mult,
             )
-            inv_ps[t] = bank(4 + t)
-            for c in range(S // P):
-                cols = slice(c * P, (c + 1) * P)
+
+        inv_t = row_tiles("inv_t", S)
+        inv_ps = []
+        for t in range(PACK):
+            nc.scalar.activation(out=inv_t[t][:], in_=sum_ps[t][:], func=ACT.Abs_reciprocal_sqrt, bias=root_bias[:])
+            inv_ps.append(bank(PACK + t))
+            for cols in blocks:
                 nc.tensor.transpose(inv_ps[t][:, cols], inv_t[t][:, cols], ident[:])
 
-        def make_z(t):
-            scalar_gather(y_n2[t], y[t], n2_sb, S)
-            nc.vector.scalar_tensor_tensor(
-                out=z_rows[:, t, :], in0=y_n2[t][:], scalar=ga_sb[:, t : t + 1], in1=inv_ps[t][:], op0=ALU.mult, op1=ALU.mult
-            )
+        z2_codes = sbuf("z2_codes", [U], U32)
+        z2_scale = sbuf("z2_scale", [U], U8)
 
-        z2_bf = {}
-        z2_codes = keep.tile([P, U], U32, align_bytes=64, name="z2_codes")
-        z2_scale = keep.tile([P, U], U8, align_bytes=64, name="z2_scale")
-        z_bf = keep.tile([P, PACK, P, PACK], BF16, align_bytes=64, name="z_bf")
-        z_codes = keep.tile([P, S], U32, align_bytes=64, name="z_codes")
-        z_scale = keep.tile([P, S], U8, align_bytes=64, name="z_scale")
-        s_sb = row_tiles("s", U, F32)
-        s_n4 = row_tiles("sn4", U, F32)
-        res = row_tiles("res", U, F32)
-        s_ps = {}
-
-        def slots(h):
-            return slice(h * HALF_U, (h + 1) * HALF_U)
-
-        def weave_z2_vector(start, width, buffer):
-            z2_bf[start] = keep.tile([P, width, PACK], BF16, align_bytes=64, name=buffer)
-            nc.vector.tensor_copy(
-                out=z2_bf[start][:].rearrange("p (c i) j -> p c j i", i=4),
-                in_=z2_rows[:, :, start : start + width].rearrange("p j (c i) -> p c j i", i=4),
-            )
-
-        def weave_z2_scalar(start, width, buffer):
-            z2_bf[start] = keep.tile([P, width, PACK], BF16, align_bytes=64, name=buffer)
-            nc.scalar.copy(
-                out=z2_bf[start][:].rearrange("p (c i) j -> p c j i", i=4),
-                in_=z2_rows[:, :, start : start + width].rearrange("p j (c i) -> p c j i", i=4),
-            )
-
-        def weave_z2_gpsimd(start, width, buffer):
-            z2_bf[start] = keep.tile([P, width, PACK], BF16, align_bytes=64, name=buffer)
-            nc.gpsimd.tensor_scalar(
-                out=z2_bf[start][:],
-                in0=z2_rows[:, :, start : start + width].rearrange("p j c -> p c j"),
-                scalar1=1.0,
-                scalar2=0.0,
-                op0=ALU.mult,
-                op1=ALU.add,
-            )
-
-        def quantize_z2(start, width):
+        def quantize_z2(woven, start, width):
             nc.vector.quantize_mx(
                 out=z2_codes[:, start : start + width].bitcast(FP8X4),
                 scales=z2_scale[:, start : start + width],
-                in_=z2_bf[start][:].rearrange("p c j -> p (c j)"),
+                in_=woven[:].rearrange("p c j -> p (c j)"),
             )
 
-        def deal_z(t, copy):
-            copy(out=z_bf[:, t].rearrange("p (m i) j -> p m j i", i=2), in_=z_src[:, t])
+        z2_woven = []
+        for n, (start, width) in enumerate(Z2_PIECES[:-1]):
+            z2_woven.append(sbuf("z2_woven%d" % n, [width, PACK], BF16))
+            nc.vector.tensor_copy(
+                out=z2_woven[n][:].rearrange("p (c i) j -> p c j i", i=4),
+                in_=z2_rows[:, :, start : start + width].rearrange("p j (c i) -> p c j i", i=4),
+            )
+        for n, (start, width) in enumerate(Z2_PIECES[:-1]):
+            quantize_z2(z2_woven[n], start, width)
+        z2_last = sbuf("z2_last", [gpsimd_width, PACK], BF16, tag="z2_woven1")
+        nc.gpsimd.tensor_scalar(
+            out=z2_last[:],
+            in0=z2_rows[:, :, gpsimd_start:U].rearrange("p j c -> p c j"),
+            scalar1=1.0,
+            scalar2=0.0,
+            op0=ALU.mult,
+            op1=ALU.add,
+        )
 
-        def quantize_z(t):
-            places = slice(t * P, (t + 1) * P)
+        z_rows = sbuf("z_rows", [PACK, S], BF16, tag="z2_woven0")
+        y_n2 = row_tiles("y_n2_", S)
+        for t in range(PACK):
+            gather_places(y_n2[t], y[t], n2_sb)
+            nc.vector.scalar_tensor_tensor(
+                out=z_rows[:, t, :],
+                in0=y_n2[t][:],
+                scalar=ga_sb[:, t : t + 1],
+                in1=inv_ps[t][:],
+                op0=ALU.mult,
+                op1=ALU.mult,
+            )
+        quantize_z2(z2_last, gpsimd_start, gpsimd_width)
+
+        z_dealt = z_rows[:].rearrange("p j (m i r) -> p r m j i", i=2, r=PACK)
+        z_woven = [sbuf("z_woven%d" % r, [P, PACK], BF16) for r in range(PACK)]
+        z_codes = sbuf("z_codes", [S], U32)
+        z_scale = sbuf("z_scale", [S], U8)
+        s_sb = row_tiles("s", U)
+        s_ps = {}
+
+        def weave_z(r, copy):
+            copy(out=z_woven[r][:].rearrange("p (m i) j -> p m j i", i=2), in_=z_dealt[:, r])
+
+        def quantize_z(r):
             nc.vector.quantize_mx(
-                out=z_codes[:, places].bitcast(FP8X4),
-                scales=z_scale[:, places],
-                in_=z_bf[:, t].rearrange("p m j -> p (m j)"),
+                out=z_codes[:, blocks[r]].bitcast(FP8X4),
+                scales=z_scale[:, blocks[r]],
+                in_=z_woven[r][:].rearrange("p m j -> p (m j)"),
             )
 
-        def scores(t, start, width, b):
-            places = slice(t * P, (t + 1) * P)
-            s_ps[t, start] = bank(b)
+        def scores(r, start, width, b):
+            s_ps[r, start] = bank(b)[:, 0:width]
             nc.tensor.matmul_mx(
-                out=s_ps[t, start][:, 0:width],
-                lhsT=z_codes[:, places].bitcast(FP8X4),
-                lhsT_scale=z_scale[:, places],
+                out=s_ps[r, start],
+                lhsT=z_codes[:, blocks[r]].bitcast(FP8X4),
+                lhsT_scale=z_scale[:, blocks[r]],
                 rhs=z2_codes[:, start : start + width].bitcast(FP8X4),
                 rhs_scale=z2_scale[:, start : start + width],
                 start=True,
                 stop=True,
             )
 
-        def empty_scalar(t, start, lo, hi):
-            nc.scalar.activation(
-                out=s_sb[t][:, start + lo : start + hi], in_=s_ps[t, start][:, lo:hi], func=ACT.Copy, scale=0.0625
-            )
+        def empty_scalar(r, start, width):
+            nc.scalar.activation(out=s_sb[r][:, start : start + width], in_=s_ps[r, start], func=ACT.Copy, scale=0.0625)
 
-        def empty_vector(t, start, lo, hi):
+        def empty_vector(r, start, width):
             nc.vector.tensor_scalar(
-                out=s_sb[t][:, start + lo : start + hi], in0=s_ps[t, start][:, lo:hi], scalar1=0.0625, scalar2=None, op0=ALU.mult
+                out=s_sb[r][:, start : start + width], in0=s_ps[r, start], scalar1=0.0625, scalar2=None, op0=ALU.mult
             )
 
-        def finish(t, widths):
+        weave_z(0, nc.vector.tensor_copy)
+        quantize_z(0)
+        for q, b in enumerate((0, PACK, last, PACK + last)):
+            scores(0, q * QUARTER_U, QUARTER_U, b)
+        for q in range(U // QUARTER_U):
+            (empty_vector if q % 2 else empty_scalar)(0, q * QUARTER_U, QUARTER_U)
+        for r in reversed(range(1, PACK)):
+            weave_z(r, nc.scalar.copy)
+        for r in range(1, PACK):
+            quantize_z(r)
+            scores(r, 0, BANK, r)
+            scores(r, BANK, BANK, PACK + r)
+
+        s_n4 = row_tiles("s_n4_", U)
+        res = row_tiles("res", U)
+
+        def finish(r, widths):
             start = 0
             for width in widths:
                 cols = slice(start, start + width)
                 nc.scalar.activation(
-                    out=s_n4[t][:, cols], in_=s_sb[t][:].indirect(entries(n4_sb, start, width)), func=ACT.Copy
+                    out=s_n4[r][:, cols], in_=s_sb[r][:].indirect(entries(n4_sb, start, width)), func=ACT.Copy
                 )
                 nc.vector.tensor_tensor(
-                    out=res[t][:, cols],
-                    in0=s_sb[t][:].indirect(entries(n5_sb, start, width)),
-                    in1=s_n4[t][:, cols],
+                    out=res[r][:, cols],
+                    in0=s_sb[r][:].indirect(entries(n5_sb, start, width)),
+                    in1=s_n4[r][:, cols],
                     op=ALU.mult,
                 )
-                nc.sync.dma_start(out=out_rows[t][:, cols], in_=res[t][:, cols])
+                nc.sync.dma_start(out=out_rows[r][:, cols], in_=res[r][:, cols])
                 start = start + width
 
-        halves = (slice(0, HALF_S), slice(HALF_S, S))
-        whole = (slice(0, S),)
-        old[0] = tile_f32("w_raw1")
-        for h in range(2):
-            nc.vector.tensor_copy(out=old[0][:, halves[h]], in_=page[0][:].indirect(entries(n3_sb, h * HALF_S, HALF_S)))
-        sigmoid_y(0)
-        for cols in halves:
-            difference(0, cols)
-        write_page(0, nc.vector, halves)
-        fetch_old(1)
-        sigmoid_y(1)
-        difference(1, whole[0])
-        write_page(1, nc.gpsimd, whole)
-        for t in range(2, PACK):
-            sigmoid_y(t)
-            fetch_y(t, "y%d" % t, nc.scalar.copy)
-            fetch_old(t)
-            difference(t, whole[0])
-            if t == 2:
-                square_gpsimd(t, "old1")
-            write_page(t, nc.gpsimd, whole)
-        for t in range(2):
-            fetch_y(t, "y%d" % t, nc.scalar.copy)
-        square_scalar(0)
-        square_scalar(1)
-        square_vector(3, "sq3")
-        for t in range(PACK):
-            denominator(t)
-        z2_rows = keep.tile([P, PACK, U], BF16, align_bytes=64, name="step")
-        weigh_page_gpsimd(0)
-        weigh_page_gpsimd(1)
-        weigh_page_gpsimd(2)
-        weigh_page_vector(3, slice(0, 640))
-        weigh_page_vector(3, slice(640, U))
-        for t in range(PACK):
-            inverse_root(t)
-        weave_z2_vector(0, 256, "z2_bf0")
-        weave_z2_vector(256, 384, "z2_bf1")
-        quantize_z2(0, 256)
-        quantize_z2(256, 384)
-        weave_z2_gpsimd(640, 384, "z2_bf1")
-        z_rows = keep.tile([P, PACK, S], BF16, align_bytes=64, name="z2_bf0")
-        z_src = z_rows[:].rearrange("p j (m i t) -> p t m j i", i=2, t=PACK)
-        for t in range(PACK):
-            make_z(t)
-        quantize_z2(640, 384)
-        deal_z(0, nc.scalar.copy)
-        quantize_z(0)
-        for q, b in enumerate((0, 4, 3, 7)):
-            scores(0, 256 * q, 256, b)
-        for q in range(4):
-            (empty_vector if q % 2 else empty_scalar)(0, 256 * q, 0, 256)
-        for t in range(1, PACK):
-            deal_z(t, nc.vector.tensor_copy if t % 2 else nc.scalar.copy)
-            quantize_z(t)
-            scores(t, 0, 512, t)
-            scores(t, 512, 512, 4 + t)
-        empty_vector(1, 0, 0, 512)
-        empty_vector(1, 512, 0, 512)
-        empty_vector(2, 0, 0, 512)
-        empty_vector(2, 512, 0, 512)
-        finish(0, (512, 512))
-        finish(1, (512, 512))
-        empty_scalar(3, 0, 0, 512)
-        empty_scalar(3, 512, 0, 512)
-        finish(2, (512, 512))
-        finish(3, (512, 256, 256))
+        for r in (1, 2):
+            for start in (0, BANK):
+                empty_vector(r, start, BANK)
+        finish(0, OUT_PIECES)
+        finish(1, OUT_PIECES)
+        for start in (0, BANK):
+            empty_scalar(last, start, BANK)
+        finish(2, OUT_PIECES)
+        finish(last, LAST_OUT_PIECES)

from contextlib import ExitStack

import concourse.mybir as mybir
from concourse.masks import make_identity

K, T, S, H, U = 512, 2048, 512, 512, 1024
FLOPS = 2 * K * H * S + 2 * H * S * U

F32 = mybir.dt.float32
BF16 = mybir.dt.bfloat16
I32 = mybir.dt.int32
U32 = mybir.dt.uint32
U16 = mybir.dt.uint16
U8 = mybir.dt.uint8
FP8X4 = mybir.dt.float8_e4m3fn_x4
ACT = mybir.ActivationFunctionType
ALU = mybir.AluOpType

P = 128
PACK = 4
BANK = 512
LIST_COLUMN = 16
QUADRANTS = 4
HALF_H = H // 2
HALF_S = S // 2
QUARTER_U = U // 4
W_VECTOR = 44
Z2_PIECES = ((0, 256), (256, 384), (640, 384))
OUT_PIECES = (512, 512)
LAST_OUT_PIECES = (512, 256, 256)


def tile_picked_selfrmspagetprod_none_p_kernel(
    tc, x_words, x_scales, w1, mem, ga, gb, offs, n1, n2, n3, n4, n5, out
):
    nc = tc.nc
    with ExitStack() as ctx:
        lists = ctx.enter_context(tc.tile_pool(name="lists", bufs=1))
        keep = ctx.enter_context(tc.tile_pool(name="keep", bufs=1))
        psum = ctx.enter_context(tc.psum_pool(name="psum", bufs=1))

        def sbuf(name, shape, dtype, tag=""):
            return keep.tile([P] + shape, dtype, name=name, tag=tag or name, align_bytes=64)

        def row_tiles(name, width):
            return [sbuf("%s%d" % (name, t), [width], F32) for t in range(PACK)]

        def bank(b):
            return psum.tile([P, BANK], F32, name="bank%d" % b)

        def entries(list_tile, start, count):
            return list_tile[:, start // LIST_COLUMN : (start + count) // LIST_COLUMN]

        offs_sb = lists.tile([P, S // LIST_COLUMN], U16)
        n1_sb = lists.tile([P, S // LIST_COLUMN], U16)
        n2_sb = lists.tile([P, S // LIST_COLUMN], U16)
        n3_sb = lists.tile([P, S // LIST_COLUMN], U16)
        n4_sb = lists.tile([P, U // LIST_COLUMN], U16)
        n5_sb = lists.tile([P, U // LIST_COLUMN], U16)

        xw_all = sbuf("xw_all", [T], U32)
        xs_all = sbuf("xs_all", [T], U8)
        w_raw = [sbuf("w_raw%d" % h, [PACK, HALF_H], F32) for h in range(2)]
        ga_sb = keep.tile([P, PACK], F32)
        gb_sb = keep.tile([P, PACK], F32)
        page = row_tiles("page", U)
        mem_rows = mem.rearrange("(p t) w -> t p w", t=PACK)
        out_rows = out.rearrange("(p t) w -> t p w", t=PACK)

        nc.vector.memset(xs_all[:].bitcast(I32), 0)
        nc.sync.dma_start(out=offs_sb[:], in_=offs)
        nc.sync.dma_start(out=xw_all[:].bitcast(I32), in_=x_words[0].rearrange("p n r -> p (n r)").bitcast(I32))
        for q in range(QUADRANTS):
            nc.sync.dma_start(
                out=xs_all[32 * q : 32 * q + 4, :].bitcast(I32), in_=x_scales[0, 4 * q : 4 * q + 4, :].bitcast(I32)
            )
        w_rows = w1.rearrange("(p j) c -> p j c", j=PACK)
        for h in range(2):
            nc.sync.dma_start(out=w_raw[h][:], in_=w_rows[:, :, h * HALF_H : (h + 1) * HALF_H])
        nc.sync.dma_start(out=n3_sb[:], in_=n3)
        nc.sync.dma_start(out=page[0][:], in_=mem_rows[0])
        nc.sync.dma_start(out=page[1][:], in_=mem_rows[1])
        nc.sync.dma_start(out=n1_sb[:], in_=n1)
        nc.sync.dma_start(out=page[2][:], in_=mem_rows[2])
        nc.sync.dma_start(out=page[3][:], in_=mem_rows[3])
        nc.sync.dma_start(out=gb_sb[:], in_=gb.rearrange("(p t) o -> p (t o)", t=PACK))
        nc.sync.dma_start(out=ga_sb[:], in_=ga.rearrange("(p t) o -> p (t o)", t=PACK))
        nc.sync.dma_start(out=n2_sb[:], in_=n2)
        nc.sync.dma_start(out=n4_sb[:], in_=n4)
        nc.sync.dma_start(out=n5_sb[:], in_=n5)
        ident = sbuf("ident", [P], F32)
        make_identity(nc, ident[:])
        root_bias = keep.tile([P, 1], F32)
        nc.gpsimd.memset(root_bias[:], 0.25)

        w_bf = sbuf("w_bf", [PACK, P, PACK], BF16)
        w_dst = w_bf[:].rearrange("p t m j -> p m j t")
        w_src = [w_raw[h][:].rearrange("p j (m t) -> p m j t", t=PACK) for h in range(2)]
        half_m = P // 2
        xw = sbuf("xw", [S], U32)
        xs = sbuf("xs", [S], U8)
        nc.vector.tensor_copy(out=xw[:], in_=xw_all[:].indirect(offs_sb[:]))
        nc.vector.tensor_copy(out=xs[:], in_=xs_all[:].indirect(offs_sb[:]))
        nc.scalar.copy(out=w_dst[:, 0:half_m], in_=w_src[0])
        nc.vector.tensor_copy(out=w_dst[:, half_m : half_m + W_VECTOR], in_=w_src[1][:, 0:W_VECTOR])
        nc.scalar.copy(out=w_dst[:, half_m + W_VECTOR : P], in_=w_src[1][:, W_VECTOR:half_m])
        w_codes = sbuf("w_codes", [H], U32)
        w_scale = sbuf("w_scale", [H], U8)
        y_ps = [bank(PACK + t) for t in range(PACK)]
        for t in range(PACK):
            features = slice(t * P, (t + 1) * P)
            nc.vector.quantize_mx(
                out=w_codes[:, features].bitcast(FP8X4),
                scales=w_scale[:, features],
                in_=w_bf[:, t].rearrange("p m j -> p (m j)"),
            )
            nc.tensor.matmul_mx(
                out=y_ps[t][:],
                lhsT=w_codes[:, features].bitcast(FP8X4),
                lhsT_scale=w_scale[:, features],
                rhs=xw[:].bitcast(FP8X4),
                rhs_scale=xs[:],
                start=True,
                stop=True,
            )

        y = row_tiles("y", S)
        gate = row_tiles("gate", S)
        diff = row_tiles("diff", S)
        new = row_tiles("new", S)
        old = {}
        sq = {}
        halves = [slice(h * HALF_S, (h + 1) * HALF_S) for h in range(2)]
        whole = [slice(0, S)]

        def sigmoid_y(t):
            nc.scalar.activation(out=gate[t][:], in_=y_ps[t][:], func=ACT.Sigmoid)

        def copy_y(t):
            nc.scalar.copy(out=y[t][:], in_=y_ps[t][:])

        def fetch_old(t):
            old[t] = sbuf("old%d" % t, [S], F32)
            nc.scalar.activation(out=old[t][:], in_=page[t][:].indirect(n3_sb[:]), func=ACT.Copy)

        def difference(t, pieces):
            for cols in pieces:
                nc.vector.tensor_tensor(
                    out=diff[t][:, cols], in0=y_ps[t][:, cols], in1=old[t][:, cols], op=ALU.subtract
                )

        def write_page(t, engine, pieces):
            step = sbuf("step%d" % t, [S], F32, tag="step")
            for cols in pieces:
                engine.tensor_tensor(out=step[:, cols], in0=diff[t][:, cols], in1=gate[t][:, cols], op=ALU.mult)
            for cols in pieces:
                engine.tensor_tensor(out=new[t][:, cols], in0=step[:, cols], in1=old[t][:, cols], op=ALU.add)
            nc.vector.tensor_copy(out=page[t][:].indirect(n3_sb[:]), in_=new[t][:])

        old[0] = sbuf("old0", [S], F32, tag="w_raw1")
        for h in range(2):
            nc.vector.tensor_copy(
                out=old[0][:, halves[h]], in_=page[0][:].indirect(entries(n3_sb, h * HALF_S, HALF_S))
            )
        sigmoid_y(0)
        difference(0, halves)
        write_page(0, nc.vector, halves)
        fetch_old(1)
        sigmoid_y(1)
        difference(1, whole)
        write_page(1, nc.gpsimd, whole)
        sigmoid_y(2)
        copy_y(2)
        fetch_old(2)
        difference(2, whole)
        sq[2] = sbuf("sq2", [S], F32, tag="old1")
        nc.gpsimd.tensor_tensor(out=sq[2][:], in0=y[2][:], in1=y[2][:], op=ALU.mult)
        write_page(2, nc.gpsimd, whole)
        sigmoid_y(3)
        copy_y(3)
        fetch_old(3)
        difference(3, whole)
        write_page(3, nc.gpsimd, whole)

        for t in range(2):
            copy_y(t)
        for t in range(2):
            sq[t] = sbuf("sq%d" % t, [S], F32)
            nc.scalar.activation(out=sq[t][:], in_=y[t][:], func=ACT.Square)
        sq[3] = sbuf("sq3", [S], F32)
        nc.vector.tensor_tensor(out=sq[3][:], in0=y_ps[3][:], in1=y[3][:], op=ALU.mult)

        def gather_places(dst, window, list_tile):
            for h in range(2):
                nc.scalar.activation(
                    out=dst[:, halves[h]], in_=window[:].indirect(entries(list_tile, h * HALF_S, HALF_S)), func=ACT.Copy
                )

        sq_n1 = row_tiles("sq_n1_", S)
        blocks = [slice(c * P, (c + 1) * P) for c in range(S // P)]
        sum_ps = []
        for t in range(PACK):
            gather_places(sq_n1[t], sq[t], n1_sb)
            sum_ps.append(bank(t))
            for cols in blocks:
                for first, term in ((True, sq[t]), (False, sq_n1[t])):
                    nc.tensor.matmul(
                        out=sum_ps[t][:, cols],
                        lhsT=term[:, cols],
                        rhs=ident[:],
                        is_transpose=True,
                        start=first,
                        stop=not first,
                    )

        z2_rows = sbuf("z2_rows", [PACK, U], BF16, tag="step")
        for t in range(PACK - 1):
            nc.gpsimd.tensor_scalar(
                out=z2_rows[:, t, :], in0=page[t][:], scalar1=gb_sb[:, t : t + 1], scalar2=0.0, op0=ALU.mult, op1=ALU.add
            )
        last = PACK - 1
        gpsimd_start, gpsimd_width = Z2_PIECES[-1]
        for cols in (slice(0, gpsimd_start), slice(gpsimd_start, U)):
            nc.vector.tensor_scalar(
                out=z2_rows[:, last, cols],
                in0=page[last][:, cols],
                scalar1=gb_sb[:, last : last + 1],
                scalar2=None,
                op0=ALU.mult,
            )

        inv_t = row_tiles("inv_t", S)
        inv_ps = []
        for t in range(PACK):
            nc.scalar.activation(out=inv_t[t][:], in_=sum_ps[t][:], func=ACT.Abs_reciprocal_sqrt, bias=root_bias[:])
            inv_ps.append(bank(PACK + t))
            for cols in blocks:
                nc.tensor.transpose(inv_ps[t][:, cols], inv_t[t][:, cols], ident[:])

        z2_codes = sbuf("z2_codes", [U], U32)
        z2_scale = sbuf("z2_scale", [U], U8)

        def quantize_z2(woven, start, width):
            nc.vector.quantize_mx(
                out=z2_codes[:, start : start + width].bitcast(FP8X4),
                scales=z2_scale[:, start : start + width],
                in_=woven[:].rearrange("p c j -> p (c j)"),
            )

        z2_woven = []
        for n, (start, width) in enumerate(Z2_PIECES[:-1]):
            z2_woven.append(sbuf("z2_woven%d" % n, [width, PACK], BF16))
            nc.vector.tensor_copy(
                out=z2_woven[n][:].rearrange("p (c i) j -> p c j i", i=4),
                in_=z2_rows[:, :, start : start + width].rearrange("p j (c i) -> p c j i", i=4),
            )
        for n, (start, width) in enumerate(Z2_PIECES[:-1]):
            quantize_z2(z2_woven[n], start, width)
        z2_last = sbuf("z2_last", [gpsimd_width, PACK], BF16, tag="z2_woven1")
        nc.gpsimd.tensor_scalar(
            out=z2_last[:],
            in0=z2_rows[:, :, gpsimd_start:U].rearrange("p j c -> p c j"),
            scalar1=1.0,
            scalar2=0.0,
            op0=ALU.mult,
            op1=ALU.add,
        )

        z_rows = sbuf("z_rows", [PACK, S], BF16, tag="z2_woven0")
        y_n2 = row_tiles("y_n2_", S)
        for t in range(PACK):
            gather_places(y_n2[t], y[t], n2_sb)
            nc.vector.scalar_tensor_tensor(
                out=z_rows[:, t, :],
                in0=y_n2[t][:],
                scalar=ga_sb[:, t : t + 1],
                in1=inv_ps[t][:],
                op0=ALU.mult,
                op1=ALU.mult,
            )
        quantize_z2(z2_last, gpsimd_start, gpsimd_width)

        z_dealt = z_rows[:].rearrange("p j (m i r) -> p r m j i", i=2, r=PACK)
        z_woven = [sbuf("z_woven%d" % r, [P, PACK], BF16) for r in range(PACK)]
        z_codes = sbuf("z_codes", [S], U32)
        z_scale = sbuf("z_scale", [S], U8)
        s_sb = row_tiles("s", U)
        s_ps = {}

        def weave_z(r, copy):
            copy(out=z_woven[r][:].rearrange("p (m i) j -> p m j i", i=2), in_=z_dealt[:, r])

        def quantize_z(r):
            nc.vector.quantize_mx(
                out=z_codes[:, blocks[r]].bitcast(FP8X4),
                scales=z_scale[:, blocks[r]],
                in_=z_woven[r][:].rearrange("p m j -> p (m j)"),
            )

        def scores(r, start, width, b):
            s_ps[r, start] = bank(b)[:, 0:width]
            nc.tensor.matmul_mx(
                out=s_ps[r, start],
                lhsT=z_codes[:, blocks[r]].bitcast(FP8X4),
                lhsT_scale=z_scale[:, blocks[r]],
                rhs=z2_codes[:, start : start + width].bitcast(FP8X4),
                rhs_scale=z2_scale[:, start : start + width],
                start=True,
                stop=True,
            )

        def empty_scalar(r, start, width):
            nc.scalar.activation(out=s_sb[r][:, start : start + width], in_=s_ps[r, start], func=ACT.Copy, scale=0.0625)

        def empty_vector(r, start, width):
            nc.vector.tensor_scalar(
                out=s_sb[r][:, start : start + width], in0=s_ps[r, start], scalar1=0.0625, scalar2=None, op0=ALU.mult
            )

        weave_z(0, nc.vector.tensor_copy)
        quantize_z(0)
        for q, b in enumerate((0, PACK, last, PACK + last)):
            scores(0, q * QUARTER_U, QUARTER_U, b)
        for q in range(U // QUARTER_U):
            (empty_vector if q % 2 else empty_scalar)(0, q * QUARTER_U, QUARTER_U)
        for r in reversed(range(1, PACK)):
            weave_z(r, nc.scalar.copy)
        for r in range(1, PACK):
            quantize_z(r)
            scores(r, 0, BANK, r)
            scores(r, BANK, BANK, PACK + r)

        s_n4 = row_tiles("s_n4_", U)
        res = row_tiles("res", U)

        def finish(r, widths):
            start = 0
            for width in widths:
                cols = slice(start, start + width)
                nc.scalar.activation(
                    out=s_n4[r][:, cols], in_=s_sb[r][:].indirect(entries(n4_sb, start, width)), func=ACT.Copy
                )
                nc.vector.tensor_tensor(
                    out=res[r][:, cols],
                    in0=s_sb[r][:].indirect(entries(n5_sb, start, width)),
                    in1=s_n4[r][:, cols],
                    op=ALU.mult,
                )
                nc.sync.dma_start(out=out_rows[r][:, cols], in_=res[r][:, cols])
                start = start + width

        for r in (1, 2):
            for start in (0, BANK):
                empty_vector(r, start, BANK)
        finish(0, OUT_PIECES)
        finish(1, OUT_PIECES)
        for start in (0, BANK):
            empty_scalar(last, start, BANK)
        finish(2, OUT_PIECES)
        finish(last, LAST_OUT_PIECES)
